import numpy as np
import ml_dtypes


def mxq(x, axis, fmt="e4m3"):
    dtype, down = {"e4m3": (ml_dtypes.float8_e4m3fn, 7), "e5m2": (ml_dtypes.float8_e5m2, 14)}[fmt]
    v = np.moveaxis(np.asarray(x, np.float32).astype(ml_dtypes.bfloat16).astype(np.float64), axis, -1)
    blocks = v.reshape(v.shape[:-1] + (-1, 32))
    amax = np.abs(blocks).max(-1, keepdims=True)
    byte = np.maximum(np.where(amax > 0, np.frexp(amax)[1] - 1 + 127, 0) - down, 1)
    scale = np.exp2(byte - 127.0)
    codes = (blocks / scale).astype(np.float32).astype(dtype).astype(np.float64)
    return np.moveaxis((codes * scale).reshape(v.shape), -1, axis)


WIDE = False


def mx_kscale(k):
    if not WIDE:
        return np.ones(k)
    levels = np.array([10, -10, 5, -5, 0])
    if k % 512:
        return np.exp2(np.random.permutation(np.resize(levels, k // 32))).repeat(32)
    a = np.empty((k // 512, 16))
    for p in range(k // 512):
        a[p, :8] = np.random.permutation(np.resize(levels, 8))
        for g in range(8):
            far = levels[np.abs(levels - a[p, g]) >= 10]
            a[p, g + 8] = far[np.random.randint(len(far))]
    return np.exp2(a.ravel()).repeat(32)


def f64(x):
    return np.asarray(x).astype(np.float64)


def striped(idx):
    return np.tile(idx.reshape(-1, 16).T, (8, 1)).astype(np.uint16)


def unstriped(offs):
    return offs[:16].T.reshape(-1).astype(np.int64)


def striped8(idx):
    return np.concatenate([x.reshape(-1, 16).T for x in idx]).astype(np.uint16)


def runs(offs, k):
    lists = np.stack([offs[16 * r : 16 * r + 16].T.reshape(-1) for r in range(8)]).astype(np.int64)
    return lists[np.arange(k) % 512 // 64]


def pack_weight(w):
    k, n = w.shape
    w = f64(np.asarray(w, np.float32).astype(ml_dtypes.bfloat16)).reshape(k // 32, 32, n)
    amax = np.abs(w).max(1)
    byte = np.clip(np.where(amax > 0, np.frexp(amax)[1] - 1 + 127 - 7, 1), 1, 254)
    scaled = (w * np.exp2(127.0 - byte)[:, None, :]).reshape(k, n).astype(np.float32)
    words = np.ascontiguousarray(scaled.reshape(k // 512, 128, 4, n).transpose(0, 1, 3, 2)).astype(ml_dtypes.float8_e4m3fn).view(np.uint8)
    return words, np.ascontiguousarray(byte.astype(np.uint8).reshape(k // 512, 16, n))


def unpack_weight(words, scales):
    g, p, n, _ = words.shape
    vals = np.ascontiguousarray(words).view(ml_dtypes.float8_e4m3fn).astype(np.float64) * np.repeat(np.exp2(scales.astype(np.float64) - 127.0), 8, axis=1)[..., None]
    return vals.transpose(0, 1, 3, 2).reshape(g * 512, n)


def sigmoid(v):
    return 1.0 / (1.0 + np.exp(-np.maximum(v, -700.0)))


K, T, S, N, H, G = 512, 2048, 256, 512, 512, 2048


def setup_inputs():
    n = np.random.standard_normal
    s = mx_kscale(K)[:, None]
    u = mx_kscale(K)
    packed_xT = pack_weight(n((K, T)) * s)
    packed_dT = pack_weight(n((K, G)) / s)
    return {
        "x_words": packed_xT[0],
        "x_scales": packed_xT[1],
        "w1": (n((K, H)) / np.sqrt(K) / s).astype(np.float32),
        "d_words": packed_dT[0],
        "d_scales": packed_dT[1],
        "gn": (np.random.uniform(0.5, 1.5, (H, 1)) * u[:, None]).astype(np.float32),
        "w2": (n((H, N)) / np.sqrt(H) / u[:, None]).astype(np.float32),
        "offs": striped(np.random.permutation(T)[:S]),
        "k1": striped8(np.random.randint(0, G, (8, H))),
        "two": striped(np.random.permutation(T)[:S]),
        "n1": striped8(np.stack([np.random.permutation(S) for _ in range(8)])),
        "n2": striped8(np.stack([np.random.permutation(S) for _ in range(8)])),
        "n3": striped(np.random.permutation(S)),
        "n4": striped(np.random.permutation(S)),
    }


def reference(x_words, x_scales, w1, d_words, d_scales, gn, w2, offs, k1, two, n1, n2, n3, n4):
    xq = unpack_weight(x_words, x_scales)[:, unstriped(offs)]
    y = mxq(f64(w1), 0, "e4m3").T @ xq
    d_k1 = unpack_weight(d_words, d_scales)[np.arange(K)[:, None], runs(k1, K)]
    x_two = unpack_weight(x_words, x_scales)[:, unstriped(two)]
    d = 0.0625 * (d_k1.T @ x_two)
    z = f64(gn) * (y * (sigmoid(d[np.arange(H)[:, None], runs(n2, H)])) - (0.5 * (y[np.arange(H)[:, None], runs(n1, H)])))
    h = mxq(f64(w2), 0, "e4m3").T @ mxq(z, 0, "e4m3")
    return h * (h[:, unstriped(n3)] - h[:, unstriped(n4)])

@@ -1,0 +1,210 @@
+from contextlib import ExitStack
+
+import concourse.mybir as mybir
+
+F32 = mybir.dt.float32
+BF16 = mybir.dt.bfloat16
+I32 = mybir.dt.int32
+U32 = mybir.dt.uint32
+U16 = mybir.dt.uint16
+U8 = mybir.dt.uint8
+FP8X4 = mybir.dt.float8_e4m3fn_x4
+ALU = mybir.AluOpType
+ACT = mybir.ActivationFunctionType
+
+P = 128
+PACK = 4
+K, T, S, N, H, G = 512, 2048, 256, 512, 512, 2048
+HALF = S // 2
+FLOPS = 2 * K * H * S * 2 + 2 * H * N * S
+
+
+def tile_picked_twkeygatebwind_none_p_kernel(
+    tc, x_words, x_scales, w1, d_words, d_scales, gn, w2, offs, k1, two, n1, n2, n3, n4, out
+):
+    nc = tc.nc
+    with ExitStack() as ctx:
+        keep = ctx.enter_context(tc.tile_pool(name="keep", bufs=1))
+        reuse = ctx.enter_context(tc.tile_pool(name="reuse", bufs=1))
+        psum = ctx.enter_context(tc.psum_pool(name="psum", bufs=1))
+
+        def tile(name, shape, dtype):
+            return keep.tile(shape, dtype, name=name, align_bytes=64)
+
+        def load_list(name, src):
+            t = tile(name, list(src.shape), U16)
+            nc.sync.dma_start(out=t[:], in_=src)
+            return t
+
+        def cols16(lst, c):
+            return lst[:, c * HALF // 16 : (c + 1) * HALF // 16]
+
+        def placed(name, shape, dtype, offset):
+            return reuse.tile(shape, dtype, name=name, offset=offset, align_bytes=64)
+
+        ds_win = placed("ds_win", [P, G], U8, 0)
+        xs_win = placed("xs_win", [P, T], U8, 2048)
+        ds_plane = tile("ds_plane", [P, H], U8)
+        nc.vector.memset(ds_win[:].bitcast(I32), 0)
+        nc.vector.memset(xs_win[:].bitcast(I32), 0)
+        nc.vector.memset(ds_plane[:].bitcast(I32), 0)
+
+        k1_l = load_list("k1_l", k1)
+        offs_l = load_list("offs_l", offs)
+        two_l = load_list("two_l", two)
+        n1_l = load_list("n1_l", n1)
+        n2_l = load_list("n2_l", n2)
+        n3_l = load_list("n3_l", n3)
+        n4_l = load_list("n4_l", n4)
+        w1_raw = placed("w1_raw", [P, PACK, H], F32, 16384)
+        nc.sync.dma_start(out=w1_raw[:], in_=w1.rearrange("(p j) c -> p j c", j=PACK))
+        xw_win = placed("xw_win", [P, T], U32, 8192)
+        nc.sync.dma_start(out=xw_win[:].bitcast(I32), in_=x_words[0].rearrange("p n t -> p (n t)").bitcast(I32))
+        dw_win = tile("dw_win", [P, G], U32)
+        nc.sync.dma_start(out=dw_win[:].bitcast(I32), in_=d_words[0].rearrange("p n t -> p (n t)").bitcast(I32))
+        nc.scalar.dma_start(out=ds_win[0:P:8, :].bitcast(I32), in_=d_scales[0].bitcast(I32))
+        for q in range(4):
+            nc.scalar.dma_start(
+                out=xs_win[32 * q : 32 * q + 4, :].bitcast(I32), in_=x_scales[0, 4 * q : 4 * q + 4, :].bitcast(I32)
+            )
+        gn_t = tile("gn_t", [P, PACK], F32)
+        nc.gpsimd.dma_start(out=gn_t[:], in_=gn.rearrange("(p t) o -> p (t o)", t=PACK))
+        half_gn = tile("half_gn", [P, PACK], F32)
+        nc.gpsimd.tensor_scalar(out=half_gn[:], in0=gn_t[:], scalar1=0.5, scalar2=0.0, op0=ALU.mult, op1=ALU.add)
+
+        ds_got = tile("ds_got", [P, H], U8)
+        nc.vector.tensor_copy(out=ds_got[:], in_=ds_win[:].indirect(k1_l[:]))
+        ds_dealt = tile("ds_dealt", [P, H], U8)
+        nc.vector.tensor_copy(
+            out=ds_dealt[:].rearrange("p (t m) -> p m t", t=PACK), in_=ds_got[:].rearrange("p (m t) -> p m t", t=PACK)
+        )
+        xs_offs = tile("xs_offs", [P, S], U8)
+        nc.vector.tensor_copy(out=xs_offs[:], in_=xs_win[:].indirect(offs_l[:]))
+        xs_two = tile("xs_two", [P, S], U8)
+        nc.vector.tensor_copy(out=xs_two[:], in_=xs_win[:].indirect(two_l[:]))
+
+        w1_bf = tile("w1_bf", [P, H * PACK], BF16)
+        nc.scalar.activation(
+            out=w1_bf[:].rearrange("p (t m j) -> p m j t", t=PACK, j=PACK),
+            in_=w1_raw[:].rearrange("p j (m t) -> p m j t", t=PACK),
+            func=ACT.Copy,
+        )
+        w2_view = w2.rearrange("(p j) c -> p j c", j=PACK)
+        w2_raw = [placed(f"w2_raw{hf}", [P, PACK, N // 2], F32, 16384 + hf * 4096) for hf in range(2)]
+        nc.sync.dma_start(out=w2_raw[0][:, 0:2, :], in_=w2_view[:, 0:2, 0 : N // 2])
+        nc.sync.dma_start(out=w2_raw[0][:, 2:4, :], in_=w2_view[:, 2:4, 0 : N // 2])
+        nc.sync.dma_start(out=w2_raw[1][:], in_=w2_view[:, :, N // 2 : N])
+        for s in range(4):
+            nc.scalar.dma_start(out=ds_plane[s:P:32, :].bitcast(I32), in_=ds_dealt[8 * s : P : 32, :].bitcast(I32))
+        w1_codes = placed("w1_codes", [P, H], U32, 2560)
+        w1_sc = tile("w1_sc", [P, H], U8)
+        xw_offs = placed("xw_offs", [P, S], U32, 1536)
+        nc.vector.tensor_copy(out=xw_offs[:], in_=xw_win[:].indirect(offs_l[:]))
+        for hf in range(2):
+            cs = slice(hf * 256, (hf + 1) * 256)
+            nc.vector.quantize_mx(
+                out=w1_codes[:, cs].bitcast(FP8X4), scales=w1_sc[:, cs], in_=w1_bf[:, hf * 1024 : (hf + 1) * 1024]
+            )
+        xw_two = tile("xw_two", [P, S], U32)
+        nc.vector.tensor_copy(out=xw_two[:], in_=xw_win[:].indirect(two_l[:]))
+
+        y_sb = []
+        y_got = tile("y_got", [P, PACK, S], F32)
+        for t in range(PACK):
+            cs = slice(t * P, (t + 1) * P)
+            acc = psum.tile([P, 512], F32, name=f"y_acc{t}", tag=f"bank{t}")
+            nc.tensor.matmul_mx(
+                out=acc[:, 0:S], lhsT=w1_codes[:, cs].bitcast(FP8X4), lhsT_scale=w1_sc[:, cs],
+                rhs=xw_offs[:].bitcast(FP8X4), rhs_scale=xs_offs[:], start=True, stop=True,
+            )
+            y_t = tile(f"y_sb{t}", [P, S], F32)
+            nc.scalar.activation(out=y_t[:], in_=acc[:, 0:S], func=ACT.Copy, scale=half_gn[:, t : t + 1])
+            y_sb.append(y_t)
+            for c in range(2):
+                nc.scalar.activation(
+                    out=y_got[:, t, c * HALF : (c + 1) * HALF], in_=y_t[:].indirect(cols16(n1_l, c)), func=ACT.Copy
+                )
+
+        dw_got = placed("dw_got", [P, H], U32, 8192)
+        nc.vector.tensor_copy(out=dw_got[:], in_=dw_win[:].indirect(k1_l[:]))
+        dw_dealt = tile("dw_dealt", [P, H], U32)
+        nc.vector.tensor_copy(
+            out=dw_dealt[:].rearrange("p (t m) -> p m t", t=PACK), in_=dw_got[:].rearrange("p (m t) -> p m t", t=PACK)
+        )
+        th_sb = []
+        th_got = tile("th_got", [P, PACK, S], F32)
+
+        def fetch_gate(t, c):
+            nc.scalar.activation(
+                out=th_got[:, t, c * HALF : (c + 1) * HALF], in_=th_sb[t][:].indirect(cols16(n2_l, c)), func=ACT.Copy
+            )
+
+        for t in range(PACK):
+            cs = slice(t * P, (t + 1) * P)
+            acc = psum.tile([P, 512], F32, name=f"d_acc{t}", tag=f"bank{PACK + t}")
+            nc.tensor.matmul_mx(
+                out=acc[:, 0:S], lhsT=dw_dealt[:, cs].bitcast(FP8X4), lhsT_scale=ds_plane[:, cs],
+                rhs=xw_two[:].bitcast(FP8X4), rhs_scale=xs_two[:], start=True, stop=True,
+            )
+            th_t = tile(f"th_sb{t}", [P, S], F32)
+            nc.scalar.activation(out=th_t[:], in_=acc[:, 0:S], func=ACT.Tanh, scale=0.0625 * 0.5)
+            th_sb.append(th_t)
+            fetch_gate(t, 0)
+        for t in range(PACK):
+            fetch_gate(t, 1)
+
+        w2_codes = tile("w2_codes", [P, N], U32)
+        w2_sc = tile("w2_sc", [P, N], U8)
+        w2_bf = []
+        for hf in range(2):
+            bf = tile(f"w2_bf{hf}", [P, N // 2 * PACK], BF16)
+            nc.vector.tensor_copy(
+                out=bf[:].rearrange("p (c i j) -> p c j i", i=4, j=PACK),
+                in_=w2_raw[hf][:].rearrange("p j (c i) -> p c j i", i=4),
+            )
+            w2_bf.append(bf)
+        for hf in range(2):
+            cs = slice(hf * 256, (hf + 1) * 256)
+            nc.vector.quantize_mx(out=w2_codes[:, cs].bitcast(FP8X4), scales=w2_sc[:, cs], in_=w2_bf[hf][:])
+
+        gated = tile("gated", [P, PACK, S], F32)
+        h_acc = [psum.tile([P, 512], F32, name=f"h_acc{m}", tag=f"bank{m}") for m in range(4)]
+        for c in range(2):
+            js = slice(c * HALF, (c + 1) * HALF)
+            for t in range(PACK):
+                nc.vector.scalar_tensor_tensor(
+                    out=gated[:, t, js], in0=th_got[:, t, js], scalar=1.0, in1=y_sb[t][:, js], op0=ALU.add, op1=ALU.mult
+                )
+            z_bf = tile(f"z_bf{c}", [P, HALF * PACK], BF16)
+            nc.vector.tensor_tensor(
+                out=z_bf[:].rearrange("p (c i t) -> p c t i", i=4, t=PACK),
+                in0=gated[:, :, js].rearrange("p t (c i) -> p c t i", i=4),
+                in1=y_got[:, :, js].rearrange("p t (c i) -> p c t i", i=4),
+                op=ALU.subtract,
+            )
+            z_codes = tile(f"z_codes{c}", [P, HALF], U32)
+            z_sc = tile(f"z_sc{c}", [P, HALF], U8)
+            nc.vector.quantize_mx(out=z_codes[:].bitcast(FP8X4), scales=z_sc[:], in_=z_bf[:])
+            for m in range(4):
+                cs = slice(m * P, (m + 1) * P)
+                nc.tensor.matmul_mx(
+                    out=h_acc[m][:, js], lhsT=w2_codes[:, cs].bitcast(FP8X4), lhsT_scale=w2_sc[:, cs],
+                    rhs=z_codes[:].bitcast(FP8X4), rhs_scale=z_sc[:], start=True, stop=True,
+                )
+
+        for m in range(4):
+            h_t = tile(f"h_sb{m}", [P, S], F32)
+            nc.scalar.activation(out=h_t[:], in_=h_acc[m][:, 0:S], func=ACT.Copy)
+            h3 = tile(f"h3_{m}", [P, S], F32)
+            diff = tile(f"diff{m}", [P, S], F32)
+            res = tile(f"res{m}", [P, S], F32)
+            for c in range(2):
+                js = slice(c * HALF, (c + 1) * HALF)
+                nc.scalar.activation(out=h3[:, js], in_=h_t[:].indirect(cols16(n3_l, c)), func=ACT.Copy)
+                nc.vector.tensor_tensor(
+                    out=diff[:, js], in0=h_t[:].indirect(cols16(n4_l, c)), in1=h3[:, js], op=ALU.subtract
+                )
+            nc.vector.scalar_tensor_tensor(
+                out=res[:], in0=diff[:], scalar=-1.0, in1=h_t[:], op0=ALU.mult, op1=ALU.mult
+            )
+            nc.sync.dma_start(out=out[m * P : (m + 1) * P, :], in_=res[:])

@@ -16,6 +16,7 @@ P = 128
 PACK = 4
 K, T, S, N, H, G = 512, 2048, 256, 512, 512, 2048
 HALF = S // 2
+W1_SPLIT = 92
 FLOPS = 2 * K * H * S * 2 + 2 * H * N * S
 
 
@@ -39,77 +40,79 @@ def tile_picked_twkeygatebwind_none_p_kernel(
         def cols16(lst, c):
             return lst[:, c * HALF // 16 : (c + 1) * HALF // 16]
 
-        def placed(name, shape, dtype, offset):
-            return reuse.tile(shape, dtype, name=name, offset=offset, align_bytes=64)
-
-        ds_win = placed("ds_win", [P, G], U8, 0)
-        xs_win = placed("xs_win", [P, T], U8, 2048)
-        ds_plane = tile("ds_plane", [P, H], U8)
+        ds_win = tile("ds_win", [P, G], U8)
+        xs_win = tile("xs_win", [P, T], U8)
         nc.vector.memset(ds_win[:].bitcast(I32), 0)
         nc.vector.memset(xs_win[:].bitcast(I32), 0)
-        nc.vector.memset(ds_plane[:].bitcast(I32), 0)
 
         k1_l = load_list("k1_l", k1)
         offs_l = load_list("offs_l", offs)
         two_l = load_list("two_l", two)
         n1_l = load_list("n1_l", n1)
-        n2_l = load_list("n2_l", n2)
-        n3_l = load_list("n3_l", n3)
-        n4_l = load_list("n4_l", n4)
-        w1_raw = placed("w1_raw", [P, PACK, H], F32, 16384)
+        nc.sync.dma_start(out=ds_win[0:P:8, :].bitcast(I32), in_=d_scales[0].bitcast(I32))
+        w1_raw = tile("w1_raw", [P, PACK, H], F32)
         nc.sync.dma_start(out=w1_raw[:], in_=w1.rearrange("(p j) c -> p j c", j=PACK))
-        xw_win = placed("xw_win", [P, T], U32, 8192)
-        nc.sync.dma_start(out=xw_win[:].bitcast(I32), in_=x_words[0].rearrange("p n t -> p (n t)").bitcast(I32))
-        dw_win = tile("dw_win", [P, G], U32)
-        nc.sync.dma_start(out=dw_win[:].bitcast(I32), in_=d_words[0].rearrange("p n t -> p (n t)").bitcast(I32))
-        nc.scalar.dma_start(out=ds_win[0:P:8, :].bitcast(I32), in_=d_scales[0].bitcast(I32))
         for q in range(4):
-            nc.scalar.dma_start(
+            nc.sync.dma_start(
                 out=xs_win[32 * q : 32 * q + 4, :].bitcast(I32), in_=x_scales[0, 4 * q : 4 * q + 4, :].bitcast(I32)
             )
         gn_t = tile("gn_t", [P, PACK], F32)
         nc.gpsimd.dma_start(out=gn_t[:], in_=gn.rearrange("(p t) o -> p (t o)", t=PACK))
         half_gn = tile("half_gn", [P, PACK], F32)
         nc.gpsimd.tensor_scalar(out=half_gn[:], in0=gn_t[:], scalar1=0.5, scalar2=0.0, op0=ALU.mult, op1=ALU.add)
+        xw_win = tile("xw_win", [P, T], U32)
+        nc.sync.dma_start(out=xw_win[:].bitcast(I32), in_=x_words[0].rearrange("p n t -> p (n t)").bitcast(I32))
+        dw_win = tile("dw_win", [P, G], U32)
+        nc.sync.dma_start(out=dw_win[:].bitcast(I32), in_=d_words[0].rearrange("p n t -> p (n t)").bitcast(I32))
+        n2_l = load_list("n2_l", n2)
+        n3_l = load_list("n3_l", n3)
+        n4_l = load_list("n4_l", n4)
 
-        ds_got = tile("ds_got", [P, H], U8)
+        ds_got = reuse.tile([P, H], U8, name="ds_got", offset=4096 - H // 2)
         nc.vector.tensor_copy(out=ds_got[:], in_=ds_win[:].indirect(k1_l[:]))
         ds_dealt = tile("ds_dealt", [P, H], U8)
         nc.vector.tensor_copy(
             out=ds_dealt[:].rearrange("p (t m) -> p m t", t=PACK), in_=ds_got[:].rearrange("p (m t) -> p m t", t=PACK)
         )
+        w1_bf = tile("w1_bf", [P, H * PACK], BF16)
+        w1_dst = w1_bf[:].rearrange("p (t m j) -> p m j t", t=PACK, j=PACK)
+        w1_src = w1_raw[:].rearrange("p j (m t) -> p m j t", t=PACK)
+        nc.scalar.activation(out=w1_dst[:, 0:W1_SPLIT], in_=w1_src[:, 0:W1_SPLIT], func=ACT.Copy)
+        nc.vector.tensor_copy(out=w1_dst[:, W1_SPLIT:P], in_=w1_src[:, W1_SPLIT:P])
         xs_offs = tile("xs_offs", [P, S], U8)
         nc.vector.tensor_copy(out=xs_offs[:], in_=xs_win[:].indirect(offs_l[:]))
-        xs_two = tile("xs_two", [P, S], U8)
-        nc.vector.tensor_copy(out=xs_two[:], in_=xs_win[:].indirect(two_l[:]))
 
-        w1_bf = tile("w1_bf", [P, H * PACK], BF16)
-        nc.scalar.activation(
-            out=w1_bf[:].rearrange("p (t m j) -> p m j t", t=PACK, j=PACK),
-            in_=w1_raw[:].rearrange("p j (m t) -> p m j t", t=PACK),
-            func=ACT.Copy,
-        )
-        w2_view = w2.rearrange("(p j) c -> p j c", j=PACK)
-        w2_raw = [placed(f"w2_raw{hf}", [P, PACK, N // 2], F32, 16384 + hf * 4096) for hf in range(2)]
-        nc.sync.dma_start(out=w2_raw[0][:, 0:2, :], in_=w2_view[:, 0:2, 0 : N // 2])
-        nc.sync.dma_start(out=w2_raw[0][:, 2:4, :], in_=w2_view[:, 2:4, 0 : N // 2])
-        nc.sync.dma_start(out=w2_raw[1][:], in_=w2_view[:, :, N // 2 : N])
-        for s in range(4):
-            nc.scalar.dma_start(out=ds_plane[s:P:32, :].bitcast(I32), in_=ds_dealt[8 * s : P : 32, :].bitcast(I32))
-        w1_codes = placed("w1_codes", [P, H], U32, 2560)
+        for s in range(1, 4):
+            nc.sync.dma_start(out=ds_dealt[s:P:32, :].bitcast(I32), in_=ds_dealt[8 * s : P : 32, :].bitcast(I32))
+        w2_raw = []
+        for hf in range(2):
+            raw = reuse.tile([P, PACK, N // 2], F32, name=f"w2_raw{hf}", offset=hf * 4096)
+            nc.sync.dma_start(
+                out=raw[:], in_=w2.rearrange("(p j) c -> p j c", j=PACK)[:, :, hf * N // 2 : (hf + 1) * N // 2]
+            )
+            w2_raw.append(raw)
+        w1_codes = tile("w1_codes", [P, H], U32)
         w1_sc = tile("w1_sc", [P, H], U8)
-        xw_offs = placed("xw_offs", [P, S], U32, 1536)
+        xw_offs = tile("xw_offs", [P, S], U32)
         nc.vector.tensor_copy(out=xw_offs[:], in_=xw_win[:].indirect(offs_l[:]))
         for hf in range(2):
             cs = slice(hf * 256, (hf + 1) * 256)
             nc.vector.quantize_mx(
                 out=w1_codes[:, cs].bitcast(FP8X4), scales=w1_sc[:, cs], in_=w1_bf[:, hf * 1024 : (hf + 1) * 1024]
             )
+        xs_two = tile("xs_two", [P, S], U8)
+        nc.vector.tensor_copy(out=xs_two[:], in_=xs_win[:].indirect(two_l[:]))
         xw_two = tile("xw_two", [P, S], U32)
         nc.vector.tensor_copy(out=xw_two[:], in_=xw_win[:].indirect(two_l[:]))
 
         y_sb = []
         y_got = tile("y_got", [P, PACK, S], F32)
+
+        def fetch_y(t, c):
+            nc.scalar.activation(
+                out=y_got[:, t, c * HALF : (c + 1) * HALF], in_=y_sb[t][:].indirect(cols16(n1_l, c)), func=ACT.Copy
+            )
+
         for t in range(PACK):
             cs = slice(t * P, (t + 1) * P)
             acc = psum.tile([P, 512], F32, name=f"y_acc{t}", tag=f"bank{t}")
@@ -118,14 +121,16 @@ def tile_picked_twkeygatebwind_none_p_kernel(
                 rhs=xw_offs[:].bitcast(FP8X4), rhs_scale=xs_offs[:], start=True, stop=True,
             )
             y_t = tile(f"y_sb{t}", [P, S], F32)
-            nc.scalar.activation(out=y_t[:], in_=acc[:, 0:S], func=ACT.Copy, scale=half_gn[:, t : t + 1])
-            y_sb.append(y_t)
-            for c in range(2):
-                nc.scalar.activation(
-                    out=y_got[:, t, c * HALF : (c + 1) * HALF], in_=y_t[:].indirect(cols16(n1_l, c)), func=ACT.Copy
+            if t == 0:
+                nc.scalar.activation(out=y_t[:], in_=acc[:, 0:S], func=ACT.Copy, scale=half_gn[:, t : t + 1])
+            else:
+                nc.vector.tensor_scalar(
+                    out=y_t[:], in0=acc[:, 0:S], scalar1=half_gn[:, t : t + 1], scalar2=None, op0=ALU.mult
                 )
+            y_sb.append(y_t)
+            fetch_y(t, 0)
 
-        dw_got = placed("dw_got", [P, H], U32, 8192)
+        dw_got = tile("dw_got", [P, H], U32)
         nc.vector.tensor_copy(out=dw_got[:], in_=dw_win[:].indirect(k1_l[:]))
         dw_dealt = tile("dw_dealt", [P, H], U32)
         nc.vector.tensor_copy(
@@ -143,7 +148,7 @@ def tile_picked_twkeygatebwind_none_p_kernel(
             cs = slice(t * P, (t + 1) * P)
             acc = psum.tile([P, 512], F32, name=f"d_acc{t}", tag=f"bank{PACK + t}")
             nc.tensor.matmul_mx(
-                out=acc[:, 0:S], lhsT=dw_dealt[:, cs].bitcast(FP8X4), lhsT_scale=ds_plane[:, cs],
+                out=acc[:, 0:S], lhsT=dw_dealt[:, cs].bitcast(FP8X4), lhsT_scale=ds_dealt[:, cs],
                 rhs=xw_two[:].bitcast(FP8X4), rhs_scale=xs_two[:], start=True, stop=True,
             )
             th_t = tile(f"th_sb{t}", [P, S], F32)
@@ -152,12 +157,14 @@ def tile_picked_twkeygatebwind_none_p_kernel(
             fetch_gate(t, 0)
         for t in range(PACK):
             fetch_gate(t, 1)
+        for t in range(PACK):
+            fetch_y(t, 1)
 
         w2_codes = tile("w2_codes", [P, N], U32)
         w2_sc = tile("w2_sc", [P, N], U8)
         w2_bf = []
         for hf in range(2):
-            bf = tile(f"w2_bf{hf}", [P, N // 2 * PACK], BF16)
+            bf = reuse.tile([P, N // 2 * PACK], BF16, name=f"w2_bf{hf}", offset=8192 + hf * 2048, align_bytes=64)
             nc.vector.tensor_copy(
                 out=bf[:].rearrange("p (c i j) -> p c j i", i=4, j=PACK),
                 in_=w2_raw[hf][:].rearrange("p j (c i) -> p c j i", i=4),
@@ -167,7 +174,7 @@ def tile_picked_twkeygatebwind_none_p_kernel(
             cs = slice(hf * 256, (hf + 1) * 256)
             nc.vector.quantize_mx(out=w2_codes[:, cs].bitcast(FP8X4), scales=w2_sc[:, cs], in_=w2_bf[hf][:])
 
-        gated = tile("gated", [P, PACK, S], F32)
+        gated = reuse.tile([P, PACK, S], F32, name="gated", offset=8192)
         h_acc = [psum.tile([P, 512], F32, name=f"h_acc{m}", tag=f"bank{m}") for m in range(4)]
         for c in range(2):
             js = slice(c * HALF, (c + 1) * HALF)
@@ -194,16 +201,27 @@ def tile_picked_twkeygatebwind_none_p_kernel(
 
         for m in range(4):
             h_t = tile(f"h_sb{m}", [P, S], F32)
-            nc.scalar.activation(out=h_t[:], in_=h_acc[m][:, 0:S], func=ACT.Copy)
+            if m == 1:
+                nc.vector.tensor_copy(out=h_t[:], in_=h_acc[m][:, 0:S])
+            else:
+                nc.scalar.activation(out=h_t[:], in_=h_acc[m][:, 0:S], func=ACT.Copy)
             h3 = tile(f"h3_{m}", [P, S], F32)
             diff = tile(f"diff{m}", [P, S], F32)
             res = tile(f"res{m}", [P, S], F32)
-            for c in range(2):
-                js = slice(c * HALF, (c + 1) * HALF)
-                nc.scalar.activation(out=h3[:, js], in_=h_t[:].indirect(cols16(n3_l, c)), func=ACT.Copy)
-                nc.vector.tensor_tensor(
-                    out=diff[:, js], in0=h_t[:].indirect(cols16(n4_l, c)), in1=h3[:, js], op=ALU.subtract
-                )
+            if m < 3:
+                for c in range(2):
+                    js = slice(c * HALF, (c + 1) * HALF)
+                    nc.scalar.activation(out=h3[:, js], in_=h_t[:].indirect(cols16(n3_l, c)), func=ACT.Copy)
+                    nc.vector.tensor_tensor(
+                        out=diff[:, js], in0=h_t[:].indirect(cols16(n4_l, c)), in1=h3[:, js], op=ALU.subtract
+                    )
+            else:
+                h4 = tile("h4", [P, S], F32)
+                for c in range(2):
+                    js = slice(c * HALF, (c + 1) * HALF)
+                    nc.scalar.activation(out=h3[:, js], in_=h_t[:].indirect(cols16(n3_l, c)), func=ACT.Copy)
+                    nc.scalar.activation(out=h4[:, js], in_=h_t[:].indirect(cols16(n4_l, c)), func=ACT.Copy)
+                    nc.vector.tensor_tensor(out=diff[:, js], in0=h4[:, js], in1=h3[:, js], op=ALU.subtract)
             nc.vector.scalar_tensor_tensor(
                 out=res[:], in0=diff[:], scalar=-1.0, in1=h_t[:], op0=ALU.mult, op1=ALU.mult
             )

@@ -45,6 +45,14 @@ def tile_picked_twkeygatebwind_none_p_kernel(
         nc.vector.memset(ds_win[:].bitcast(I32), 0)
         nc.vector.memset(xs_win[:].bitcast(I32), 0)
 
+        gn_t = tile("gn_t", [P, PACK], F32)
+        nc.gpsimd.dma_start(out=gn_t[:], in_=gn.rearrange("(p t) o -> p (t o)", t=PACK))
+        half_gn = tile("half_gn", [P, PACK], F32)
+        nc.gpsimd.tensor_scalar(out=half_gn[:], in0=gn_t[:], scalar1=0.5, scalar2=0.0, op0=ALU.mult, op1=ALU.add)
+        win = [tile(f"win{t}", [P, 2 * S], F32) for t in range(PACK)]
+        for t in range(PACK):
+            nc.vector.memset(win[t][:, S : 2 * S], 0.0)
+
         k1_l = load_list("k1_l", k1)
         offs_l = load_list("offs_l", offs)
         two_l = load_list("two_l", two)
@@ -56,10 +64,6 @@ def tile_picked_twkeygatebwind_none_p_kernel(
             nc.sync.dma_start(
                 out=xs_win[32 * q : 32 * q + 4, :].bitcast(I32), in_=x_scales[0, 4 * q : 4 * q + 4, :].bitcast(I32)
             )
-        gn_t = tile("gn_t", [P, PACK], F32)
-        nc.gpsimd.dma_start(out=gn_t[:], in_=gn.rearrange("(p t) o -> p (t o)", t=PACK))
-        half_gn = tile("half_gn", [P, PACK], F32)
-        nc.gpsimd.tensor_scalar(out=half_gn[:], in0=gn_t[:], scalar1=0.5, scalar2=0.0, op0=ALU.mult, op1=ALU.add)
         xw_win = tile("xw_win", [P, T], U32)
         nc.sync.dma_start(out=xw_win[:].bitcast(I32), in_=x_words[0].rearrange("p n t -> p (n t)").bitcast(I32))
         dw_win = tile("dw_win", [P, G], U32)
@@ -74,6 +78,8 @@ def tile_picked_twkeygatebwind_none_p_kernel(
         nc.vector.tensor_copy(
             out=ds_dealt[:].rearrange("p (t m) -> p m t", t=PACK), in_=ds_got[:].rearrange("p (m t) -> p m t", t=PACK)
         )
+        ds_plane = tile("ds_plane", [P, H], U8)
+        nc.vector.tensor_copy(out=ds_plane[:].bitcast(I32), in_=ds_dealt[:].bitcast(I32))
         w1_bf = tile("w1_bf", [P, H * PACK], BF16)
         w1_dst = w1_bf[:].rearrange("p (t m j) -> p m j t", t=PACK, j=PACK)
         w1_src = w1_raw[:].rearrange("p j (m t) -> p m j t", t=PACK)
@@ -83,14 +89,9 @@ def tile_picked_twkeygatebwind_none_p_kernel(
         nc.vector.tensor_copy(out=xs_offs[:], in_=xs_win[:].indirect(offs_l[:]))
 
         for s in range(1, 4):
-            nc.sync.dma_start(out=ds_dealt[s:P:32, :].bitcast(I32), in_=ds_dealt[8 * s : P : 32, :].bitcast(I32))
-        w2_raw = []
-        for hf in range(2):
-            raw = reuse.tile([P, PACK, N // 2], F32, name=f"w2_raw{hf}", offset=hf * 4096)
-            nc.sync.dma_start(
-                out=raw[:], in_=w2.rearrange("(p j) c -> p j c", j=PACK)[:, :, hf * N // 2 : (hf + 1) * N // 2]
-            )
-            w2_raw.append(raw)
+            nc.sync.dma_start(out=ds_plane[s:P:32, :].bitcast(I32), in_=ds_dealt[8 * s : P : 32, :].bitcast(I32))
+        w2_raw = reuse.tile([P, PACK, N], F32, name="w2_raw", offset=0)
+        nc.sync.dma_start(out=w2_raw[:], in_=w2.rearrange("(p j) c -> p j c", j=PACK))
         w1_codes = tile("w1_codes", [P, H], U32)
         w1_sc = tile("w1_sc", [P, H], U8)
         xw_offs = tile("xw_offs", [P, S], U32)
@@ -105,13 +106,7 @@ def tile_picked_twkeygatebwind_none_p_kernel(
         xw_two = tile("xw_two", [P, S], U32)
         nc.vector.tensor_copy(out=xw_two[:], in_=xw_win[:].indirect(two_l[:]))
 
-        y_sb = []
         y_got = tile("y_got", [P, PACK, S], F32)
-
-        def fetch_y(t, c):
-            nc.scalar.activation(
-                out=y_got[:, t, c * HALF : (c + 1) * HALF], in_=y_sb[t][:].indirect(cols16(n1_l, c)), func=ACT.Copy
-            )
 
         for t in range(PACK):
             cs = slice(t * P, (t + 1) * P)
@@ -120,15 +115,14 @@ def tile_picked_twkeygatebwind_none_p_kernel(
                 out=acc[:, 0:S], lhsT=w1_codes[:, cs].bitcast(FP8X4), lhsT_scale=w1_sc[:, cs],
                 rhs=xw_offs[:].bitcast(FP8X4), rhs_scale=xs_offs[:], start=True, stop=True,
             )
-            y_t = tile(f"y_sb{t}", [P, S], F32)
-            if t == 0:
-                nc.scalar.activation(out=y_t[:], in_=acc[:, 0:S], func=ACT.Copy, scale=half_gn[:, t : t + 1])
+            y_t = win[t][:, 0:S]
+            if t < 1:
+                nc.scalar.activation(out=y_t, in_=acc[:, 0:S], func=ACT.Copy, scale=half_gn[:, t : t + 1])
             else:
                 nc.vector.tensor_scalar(
-                    out=y_t[:], in0=acc[:, 0:S], scalar1=half_gn[:, t : t + 1], scalar2=None, op0=ALU.mult
+                    out=y_t, in0=acc[:, 0:S], scalar1=half_gn[:, t : t + 1], scalar2=None, op0=ALU.mult
                 )
-            y_sb.append(y_t)
-            fetch_y(t, 0)
+            nc.scalar.activation(out=y_got[:, t, :], in_=win[t][:].indirect(n1_l[:]), func=ACT.Copy)
 
         dw_got = tile("dw_got", [P, H], U32)
         nc.vector.tensor_copy(out=dw_got[:], in_=dw_win[:].indirect(k1_l[:]))
@@ -148,7 +142,7 @@ def tile_picked_twkeygatebwind_none_p_kernel(
             cs = slice(t * P, (t + 1) * P)
             acc = psum.tile([P, 512], F32, name=f"d_acc{t}", tag=f"bank{PACK + t}")
             nc.tensor.matmul_mx(
-                out=acc[:, 0:S], lhsT=dw_dealt[:, cs].bitcast(FP8X4), lhsT_scale=ds_dealt[:, cs],
+                out=acc[:, 0:S], lhsT=dw_dealt[:, cs].bitcast(FP8X4), lhsT_scale=ds_plane[:, cs],
                 rhs=xw_two[:].bitcast(FP8X4), rhs_scale=xs_two[:], start=True, stop=True,
             )
             th_t = tile(f"th_sb{t}", [P, S], F32)
@@ -157,8 +151,6 @@ def tile_picked_twkeygatebwind_none_p_kernel(
             fetch_gate(t, 0)
         for t in range(PACK):
             fetch_gate(t, 1)
-        for t in range(PACK):
-            fetch_y(t, 1)
 
         w2_codes = tile("w2_codes", [P, N], U32)
         w2_sc = tile("w2_sc", [P, N], U8)
@@ -167,7 +159,7 @@ def tile_picked_twkeygatebwind_none_p_kernel(
             bf = reuse.tile([P, N // 2 * PACK], BF16, name=f"w2_bf{hf}", offset=8192 + hf * 2048, align_bytes=64)
             nc.vector.tensor_copy(
                 out=bf[:].rearrange("p (c i j) -> p c j i", i=4, j=PACK),
-                in_=w2_raw[hf][:].rearrange("p j (c i) -> p c j i", i=4),
+                in_=w2_raw[:, :, hf * N // 2 : (hf + 1) * N // 2].rearrange("p j (c i) -> p c j i", i=4),
             )
             w2_bf.append(bf)
         for hf in range(2):
@@ -175,12 +167,12 @@ def tile_picked_twkeygatebwind_none_p_kernel(
             nc.vector.quantize_mx(out=w2_codes[:, cs].bitcast(FP8X4), scales=w2_sc[:, cs], in_=w2_bf[hf][:])
 
         gated = reuse.tile([P, PACK, S], F32, name="gated", offset=8192)
-        h_acc = [psum.tile([P, 512], F32, name=f"h_acc{m}", tag=f"bank{m}") for m in range(4)]
+        h_acc = []
         for c in range(2):
             js = slice(c * HALF, (c + 1) * HALF)
             for t in range(PACK):
                 nc.vector.scalar_tensor_tensor(
-                    out=gated[:, t, js], in0=th_got[:, t, js], scalar=1.0, in1=y_sb[t][:, js], op0=ALU.add, op1=ALU.mult
+                    out=gated[:, t, js], in0=th_got[:, t, js], scalar=1.0, in1=win[t][:, js], op0=ALU.add, op1=ALU.mult
                 )
             z_bf = tile(f"z_bf{c}", [P, HALF * PACK], BF16)
             nc.vector.tensor_tensor(
@@ -194,35 +186,34 @@ def tile_picked_twkeygatebwind_none_p_kernel(
             nc.vector.quantize_mx(out=z_codes[:].bitcast(FP8X4), scales=z_sc[:], in_=z_bf[:])
             for m in range(4):
                 cs = slice(m * P, (m + 1) * P)
+                acc = psum.tile([P, 512], F32, name=f"h_acc{c}_{m}", tag=f"bank{PACK * c + m}")
+                h_acc.append(acc)
                 nc.tensor.matmul_mx(
-                    out=h_acc[m][:, js], lhsT=w2_codes[:, cs].bitcast(FP8X4), lhsT_scale=w2_sc[:, cs],
+                    out=acc[:, 0:HALF], lhsT=w2_codes[:, cs].bitcast(FP8X4), lhsT_scale=w2_sc[:, cs],
                     rhs=z_codes[:].bitcast(FP8X4), rhs_scale=z_sc[:], start=True, stop=True,
                 )
 
         for m in range(4):
-            h_t = tile(f"h_sb{m}", [P, S], F32)
+            nc.scalar.activation(out=win[m][:, 0:HALF], in_=h_acc[m][:, 0:HALF], func=ACT.Copy)
+        for m in range(4):
             if m == 1:
-                nc.vector.tensor_copy(out=h_t[:], in_=h_acc[m][:, 0:S])
+                nc.vector.tensor_copy(out=win[m][:, HALF:S], in_=h_acc[4 + m][:, 0:HALF])
             else:
-                nc.scalar.activation(out=h_t[:], in_=h_acc[m][:, 0:S], func=ACT.Copy)
+                nc.scalar.activation(out=win[m][:, HALF:S], in_=h_acc[4 + m][:, 0:HALF], func=ACT.Copy)
             h3 = tile(f"h3_{m}", [P, S], F32)
             diff = tile(f"diff{m}", [P, S], F32)
             res = tile(f"res{m}", [P, S], F32)
-            if m < 3:
-                for c in range(2):
-                    js = slice(c * HALF, (c + 1) * HALF)
-                    nc.scalar.activation(out=h3[:, js], in_=h_t[:].indirect(cols16(n3_l, c)), func=ACT.Copy)
-                    nc.vector.tensor_tensor(
-                        out=diff[:, js], in0=h_t[:].indirect(cols16(n4_l, c)), in1=h3[:, js], op=ALU.subtract
-                    )
+            nc.scalar.activation(out=h3[:], in_=win[m][:].indirect(n3_l[:]), func=ACT.Copy)
+            if m in (0, 3):
+                h4 = tile(f"h4_{m}", [P, S], F32)
+                if m == 0:
+                    nc.vector.tensor_copy(out=h4[:], in_=win[m][:].indirect(n4_l[:]))
+                else:
+                    nc.scalar.activation(out=h4[:], in_=win[m][:].indirect(n4_l[:]), func=ACT.Copy)
+                nc.vector.tensor_tensor(out=diff[:], in0=h4[:], in1=h3[:], op=ALU.subtract)
             else:
-                h4 = tile("h4", [P, S], F32)
-                for c in range(2):
-                    js = slice(c * HALF, (c + 1) * HALF)
-                    nc.scalar.activation(out=h3[:, js], in_=h_t[:].indirect(cols16(n3_l, c)), func=ACT.Copy)
-                    nc.scalar.activation(out=h4[:, js], in_=h_t[:].indirect(cols16(n4_l, c)), func=ACT.Copy)
-                    nc.vector.tensor_tensor(out=diff[:, js], in0=h4[:, js], in1=h3[:, js], op=ALU.subtract)
+                nc.vector.tensor_tensor(out=diff[:], in0=win[m][:].indirect(n4_l[:]), in1=h3[:], op=ALU.subtract)
             nc.vector.scalar_tensor_tensor(
-                out=res[:], in0=diff[:], scalar=-1.0, in1=h_t[:], op0=ALU.mult, op1=ALU.mult
+                out=res[:], in0=diff[:], scalar=-1.0, in1=win[m][:, 0:S], op0=ALU.mult, op1=ALU.mult
             )
             nc.sync.dma_start(out=out[m * P : (m + 1) * P, :], in_=res[:])

from contextlib import ExitStack

import concourse.mybir as mybir

F32 = mybir.dt.float32
BF16 = mybir.dt.bfloat16
I32 = mybir.dt.int32
U32 = mybir.dt.uint32
U16 = mybir.dt.uint16
U8 = mybir.dt.uint8
FP8X4 = mybir.dt.float8_e4m3fn_x4
ALU = mybir.AluOpType
ACT = mybir.ActivationFunctionType

P = 128
PACK = 4
K, T, S, N, H, G = 512, 2048, 256, 512, 512, 2048
HALF = S // 2
W1_SPLIT = 92
FLOPS = 2 * K * H * S * 2 + 2 * H * N * S


def tile_picked_twkeygatebwind_none_p_kernel(
    tc, x_words, x_scales, w1, d_words, d_scales, gn, w2, offs, k1, two, n1, n2, n3, n4, out
):
    nc = tc.nc
    with ExitStack() as ctx:
        keep = ctx.enter_context(tc.tile_pool(name="keep", bufs=1))
        reuse = ctx.enter_context(tc.tile_pool(name="reuse", bufs=1))
        psum = ctx.enter_context(tc.psum_pool(name="psum", bufs=1))

        def tile(name, shape, dtype):
            return keep.tile(shape, dtype, name=name, align_bytes=64)

        def load_list(name, src):
            t = tile(name, list(src.shape), U16)
            nc.sync.dma_start(out=t[:], in_=src)
            return t

        def cols16(lst, c):
            return lst[:, c * HALF // 16 : (c + 1) * HALF // 16]

        ds_win = tile("ds_win", [P, G], U8)
        xs_win = tile("xs_win", [P, T], U8)
        nc.vector.memset(ds_win[:].bitcast(I32), 0)
        nc.vector.memset(xs_win[:].bitcast(I32), 0)

        gn_t = tile("gn_t", [P, PACK], F32)
        nc.gpsimd.dma_start(out=gn_t[:], in_=gn.rearrange("(p t) o -> p (t o)", t=PACK))
        half_gn = tile("half_gn", [P, PACK], F32)
        nc.gpsimd.tensor_scalar(out=half_gn[:], in0=gn_t[:], scalar1=0.5, scalar2=0.0, op0=ALU.mult, op1=ALU.add)
        win = [tile(f"win{t}", [P, 2 * S], F32) for t in range(PACK)]
        for t in range(PACK):
            nc.vector.memset(win[t][:, S : 2 * S], 0.0)

        k1_l = load_list("k1_l", k1)
        offs_l = load_list("offs_l", offs)
        two_l = load_list("two_l", two)
        n1_l = load_list("n1_l", n1)
        nc.sync.dma_start(out=ds_win[0:P:8, :].bitcast(I32), in_=d_scales[0].bitcast(I32))
        w1_raw = tile("w1_raw", [P, PACK, H], F32)
        nc.sync.dma_start(out=w1_raw[:], in_=w1.rearrange("(p j) c -> p j c", j=PACK))
        for q in range(4):
            nc.sync.dma_start(
                out=xs_win[32 * q : 32 * q + 4, :].bitcast(I32), in_=x_scales[0, 4 * q : 4 * q + 4, :].bitcast(I32)
            )
        xw_win = tile("xw_win", [P, T], U32)
        nc.sync.dma_start(out=xw_win[:].bitcast(I32), in_=x_words[0].rearrange("p n t -> p (n t)").bitcast(I32))
        dw_win = tile("dw_win", [P, G], U32)
        nc.sync.dma_start(out=dw_win[:].bitcast(I32), in_=d_words[0].rearrange("p n t -> p (n t)").bitcast(I32))
        n2_l = load_list("n2_l", n2)
        n3_l = load_list("n3_l", n3)
        n4_l = load_list("n4_l", n4)

        ds_got = reuse.tile([P, H], U8, name="ds_got", offset=4096 - H // 2)
        nc.vector.tensor_copy(out=ds_got[:], in_=ds_win[:].indirect(k1_l[:]))
        ds_dealt = tile("ds_dealt", [P, H], U8)
        nc.vector.tensor_copy(
            out=ds_dealt[:].rearrange("p (t m) -> p m t", t=PACK), in_=ds_got[:].rearrange("p (m t) -> p m t", t=PACK)
        )
        ds_plane = tile("ds_plane", [P, H], U8)
        nc.vector.tensor_copy(out=ds_plane[:].bitcast(I32), in_=ds_dealt[:].bitcast(I32))
        w1_bf = tile("w1_bf", [P, H * PACK], BF16)
        w1_dst = w1_bf[:].rearrange("p (t m j) -> p m j t", t=PACK, j=PACK)
        w1_src = w1_raw[:].rearrange("p j (m t) -> p m j t", t=PACK)
        nc.scalar.activation(out=w1_dst[:, 0:W1_SPLIT], in_=w1_src[:, 0:W1_SPLIT], func=ACT.Copy)
        nc.vector.tensor_copy(out=w1_dst[:, W1_SPLIT:P], in_=w1_src[:, W1_SPLIT:P])
        xs_offs = tile("xs_offs", [P, S], U8)
        nc.vector.tensor_copy(out=xs_offs[:], in_=xs_win[:].indirect(offs_l[:]))

        for s in range(1, 4):
            nc.sync.dma_start(out=ds_plane[s:P:32, :].bitcast(I32), in_=ds_dealt[8 * s : P : 32, :].bitcast(I32))
        w2_raw = reuse.tile([P, PACK, N], F32, name="w2_raw", offset=0)
        nc.sync.dma_start(out=w2_raw[:], in_=w2.rearrange("(p j) c -> p j c", j=PACK))
        w1_codes = tile("w1_codes", [P, H], U32)
        w1_sc = tile("w1_sc", [P, H], U8)
        xw_offs = tile("xw_offs", [P, S], U32)
        nc.vector.tensor_copy(out=xw_offs[:], in_=xw_win[:].indirect(offs_l[:]))
        for hf in range(2):
            cs = slice(hf * 256, (hf + 1) * 256)
            nc.vector.quantize_mx(
                out=w1_codes[:, cs].bitcast(FP8X4), scales=w1_sc[:, cs], in_=w1_bf[:, hf * 1024 : (hf + 1) * 1024]
            )
        xs_two = tile("xs_two", [P, S], U8)
        nc.vector.tensor_copy(out=xs_two[:], in_=xs_win[:].indirect(two_l[:]))
        xw_two = tile("xw_two", [P, S], U32)
        nc.vector.tensor_copy(out=xw_two[:], in_=xw_win[:].indirect(two_l[:]))

        y_got = tile("y_got", [P, PACK, S], F32)

        for t in range(PACK):
            cs = slice(t * P, (t + 1) * P)
            acc = psum.tile([P, 512], F32, name=f"y_acc{t}", tag=f"bank{t}")
            nc.tensor.matmul_mx(
                out=acc[:, 0:S], lhsT=w1_codes[:, cs].bitcast(FP8X4), lhsT_scale=w1_sc[:, cs],
                rhs=xw_offs[:].bitcast(FP8X4), rhs_scale=xs_offs[:], start=True, stop=True,
            )
            y_t = win[t][:, 0:S]
            if t < 1:
                nc.scalar.activation(out=y_t, in_=acc[:, 0:S], func=ACT.Copy, scale=half_gn[:, t : t + 1])
            else:
                nc.vector.tensor_scalar(
                    out=y_t, in0=acc[:, 0:S], scalar1=half_gn[:, t : t + 1], scalar2=None, op0=ALU.mult
                )
            nc.scalar.activation(out=y_got[:, t, :], in_=win[t][:].indirect(n1_l[:]), func=ACT.Copy)

        dw_got = tile("dw_got", [P, H], U32)
        nc.vector.tensor_copy(out=dw_got[:], in_=dw_win[:].indirect(k1_l[:]))
        dw_dealt = tile("dw_dealt", [P, H], U32)
        nc.vector.tensor_copy(
            out=dw_dealt[:].rearrange("p (t m) -> p m t", t=PACK), in_=dw_got[:].rearrange("p (m t) -> p m t", t=PACK)
        )
        th_sb = []
        th_got = tile("th_got", [P, PACK, S], F32)

        def fetch_gate(t, c):
            nc.scalar.activation(
                out=th_got[:, t, c * HALF : (c + 1) * HALF], in_=th_sb[t][:].indirect(cols16(n2_l, c)), func=ACT.Copy
            )

        for t in range(PACK):
            cs = slice(t * P, (t + 1) * P)
            acc = psum.tile([P, 512], F32, name=f"d_acc{t}", tag=f"bank{PACK + t}")
            nc.tensor.matmul_mx(
                out=acc[:, 0:S], lhsT=dw_dealt[:, cs].bitcast(FP8X4), lhsT_scale=ds_plane[:, cs],
                rhs=xw_two[:].bitcast(FP8X4), rhs_scale=xs_two[:], start=True, stop=True,
            )
            th_t = tile(f"th_sb{t}", [P, S], F32)
            nc.scalar.activation(out=th_t[:], in_=acc[:, 0:S], func=ACT.Tanh, scale=0.0625 * 0.5)
            th_sb.append(th_t)
            fetch_gate(t, 0)
        for t in range(PACK):
            fetch_gate(t, 1)

        w2_codes = tile("w2_codes", [P, N], U32)
        w2_sc = tile("w2_sc", [P, N], U8)
        w2_bf = []
        for hf in range(2):
            bf = reuse.tile([P, N // 2 * PACK], BF16, name=f"w2_bf{hf}", offset=8192 + hf * 2048, align_bytes=64)
            nc.vector.tensor_copy(
                out=bf[:].rearrange("p (c i j) -> p c j i", i=4, j=PACK),
                in_=w2_raw[:, :, hf * N // 2 : (hf + 1) * N // 2].rearrange("p j (c i) -> p c j i", i=4),
            )
            w2_bf.append(bf)
        for hf in range(2):
            cs = slice(hf * 256, (hf + 1) * 256)
            nc.vector.quantize_mx(out=w2_codes[:, cs].bitcast(FP8X4), scales=w2_sc[:, cs], in_=w2_bf[hf][:])

        gated = reuse.tile([P, PACK, S], F32, name="gated", offset=8192)
        h_acc = []
        for c in range(2):
            js = slice(c * HALF, (c + 1) * HALF)
            for t in range(PACK):
                nc.vector.scalar_tensor_tensor(
                    out=gated[:, t, js], in0=th_got[:, t, js], scalar=1.0, in1=win[t][:, js], op0=ALU.add, op1=ALU.mult
                )
            z_bf = tile(f"z_bf{c}", [P, HALF * PACK], BF16)
            nc.vector.tensor_tensor(
                out=z_bf[:].rearrange("p (c i t) -> p c t i", i=4, t=PACK),
                in0=gated[:, :, js].rearrange("p t (c i) -> p c t i", i=4),
                in1=y_got[:, :, js].rearrange("p t (c i) -> p c t i", i=4),
                op=ALU.subtract,
            )
            z_codes = tile(f"z_codes{c}", [P, HALF], U32)
            z_sc = tile(f"z_sc{c}", [P, HALF], U8)
            nc.vector.quantize_mx(out=z_codes[:].bitcast(FP8X4), scales=z_sc[:], in_=z_bf[:])
            for m in range(4):
                cs = slice(m * P, (m + 1) * P)
                acc = psum.tile([P, 512], F32, name=f"h_acc{c}_{m}", tag=f"bank{PACK * c + m}")
                h_acc.append(acc)
                nc.tensor.matmul_mx(
                    out=acc[:, 0:HALF], lhsT=w2_codes[:, cs].bitcast(FP8X4), lhsT_scale=w2_sc[:, cs],
                    rhs=z_codes[:].bitcast(FP8X4), rhs_scale=z_sc[:], start=True, stop=True,
                )

        for m in range(4):
            nc.scalar.activation(out=win[m][:, 0:HALF], in_=h_acc[m][:, 0:HALF], func=ACT.Copy)
        for m in range(4):
            if m == 1:
                nc.vector.tensor_copy(out=win[m][:, HALF:S], in_=h_acc[4 + m][:, 0:HALF])
            else:
                nc.scalar.activation(out=win[m][:, HALF:S], in_=h_acc[4 + m][:, 0:HALF], func=ACT.Copy)
            h3 = tile(f"h3_{m}", [P, S], F32)
            diff = tile(f"diff{m}", [P, S], F32)
            res = tile(f"res{m}", [P, S], F32)
            nc.scalar.activation(out=h3[:], in_=win[m][:].indirect(n3_l[:]), func=ACT.Copy)
            if m in (0, 3):
                h4 = tile(f"h4_{m}", [P, S], F32)
                if m == 0:
                    nc.vector.tensor_copy(out=h4[:], in_=win[m][:].indirect(n4_l[:]))
                else:
                    nc.scalar.activation(out=h4[:], in_=win[m][:].indirect(n4_l[:]), func=ACT.Copy)
                nc.vector.tensor_tensor(out=diff[:], in0=h4[:], in1=h3[:], op=ALU.subtract)
            else:
                nc.vector.tensor_tensor(out=diff[:], in0=win[m][:].indirect(n4_l[:]), in1=h3[:], op=ALU.subtract)
            nc.vector.scalar_tensor_tensor(
                out=res[:], in0=diff[:], scalar=-1.0, in1=win[m][:, 0:S], op0=ALU.mult, op1=ALU.mult
            )
            nc.sync.dma_start(out=out[m * P : (m + 1) * P, :], in_=res[:])
